import numpy as np
import ml_dtypes


def mxq(x, axis, fmt="e4m3"):
    dtype, down = {"e4m3": (ml_dtypes.float8_e4m3fn, 7), "e5m2": (ml_dtypes.float8_e5m2, 14)}[fmt]
    v = np.moveaxis(np.asarray(x, np.float32).astype(ml_dtypes.bfloat16).astype(np.float64), axis, -1)
    blocks = v.reshape(v.shape[:-1] + (-1, 32))
    amax = np.abs(blocks).max(-1, keepdims=True)
    byte = np.maximum(np.where(amax > 0, np.frexp(amax)[1] - 1 + 127, 0) - down, 1)
    scale = np.exp2(byte - 127.0)
    codes = (blocks / scale).astype(np.float32).astype(dtype).astype(np.float64)
    return np.moveaxis((codes * scale).reshape(v.shape), -1, axis)


WIDE = False


def mx_kscale(k):
    if not WIDE:
        return np.ones(k)
    levels = np.array([10, -10, 5, -5, 0])
    if k % 512:
        return np.exp2(np.random.permutation(np.resize(levels, k // 32))).repeat(32)
    a = np.empty((k // 512, 16))
    for p in range(k // 512):
        a[p, :8] = np.random.permutation(np.resize(levels, 8))
        for g in range(8):
            far = levels[np.abs(levels - a[p, g]) >= 10]
            a[p, g + 8] = far[np.random.randint(len(far))]
    return np.exp2(a.ravel()).repeat(32)


def f64(x):
    return np.asarray(x).astype(np.float64)


def striped(idx):
    return np.tile(idx.reshape(-1, 16).T, (8, 1)).astype(np.uint16)


def unstriped(offs):
    return offs[:16].T.reshape(-1).astype(np.int64)


def pack_weight(w):
    k, n = w.shape
    w = f64(np.asarray(w, np.float32).astype(ml_dtypes.bfloat16)).reshape(k // 32, 32, n)
    amax = np.abs(w).max(1)
    byte = np.clip(np.where(amax > 0, np.frexp(amax)[1] - 1 + 127 - 7, 1), 1, 254)
    scaled = (w * np.exp2(127.0 - byte)[:, None, :]).reshape(k, n).astype(np.float32)
    words = np.ascontiguousarray(scaled.reshape(k // 512, 128, 4, n).transpose(0, 1, 3, 2)).astype(ml_dtypes.float8_e4m3fn).view(np.uint8)
    return words, np.ascontiguousarray(byte.astype(np.uint8).reshape(k // 512, 16, n))


def unpack_weight(words, scales):
    g, p, n, _ = words.shape
    vals = np.ascontiguousarray(words).view(ml_dtypes.float8_e4m3fn).astype(np.float64) * np.repeat(np.exp2(scales.astype(np.float64) - 127.0), 8, axis=1)[..., None]
    return vals.transpose(0, 1, 3, 2).reshape(g * 512, n)


def sigmoid(v):
    return 1.0 / (1.0 + np.exp(-np.maximum(v, -700.0)))


K, T, S, V = 512, 1024, 512, 256
P = 2 ** 7


def setup_inputs():
    n = np.random.standard_normal
    s = mx_kscale(K)[:, None]
    packed_xT = pack_weight(n((K, T)) * s)
    return {
        "x_words": packed_xT[0],
        "x_scales": packed_xT[1],
        "hT": (n((K, V)) / np.sqrt(K) / s).astype(np.float32),
        "gT": (n((K, V)) / np.sqrt(K) / s).astype(np.float32),
        "good": (np.tile(np.where(np.random.uniform(size=S) < 0.5, 1.0, -1.0), (P, 1))).astype(np.float32),
        "lam": (np.tile(np.random.uniform(0.5, 1.5, S), (P, 1))).astype(np.float32),
        "offs": striped(np.random.permutation(T)[:S]),
    }


def reference(x_words, x_scales, hT, gT, good, lam, offs):
    hTq = mxq(f64(hT), 0, "e4m3")
    xq = unpack_weight(x_words, x_scales)[:, unstriped(offs)]
    y = hTq.T @ xq
    ea = np.exp(y)
    sa = np.log(ea.sum(axis=1, keepdims=True))
    la = y - sa
    gTq = mxq(f64(gT), 0, "e4m3")
    z = gTq.T @ xq
    eb = np.exp(z)
    sb = np.log(eb.sum(axis=1, keepdims=True))
    lb = z - sb
    rwd = la - lb
    ad = np.abs(rwd)
    zref = ad.mean(axis=1, keepdims=True)
    val = sigmoid(1.5 * (f64(good)[:1] * (rwd - (0.3 * zref))))
    return f64(lam)[:1] * (-1.0 * val + 1.0)

@@ -1,0 +1,153 @@
+import math
+from contextlib import ExitStack
+
+import concourse.mybir as mybir
+
+F32 = mybir.dt.float32
+BF16 = mybir.dt.bfloat16
+I32 = mybir.dt.int32
+U32 = mybir.dt.uint32
+U16 = mybir.dt.uint16
+U8 = mybir.dt.uint8
+FP8X4 = mybir.dt.float8_e4m3fn_x4
+ACT = mybir.ActivationFunctionType
+ALU = mybir.AluOpType
+
+K, T, S, V = 512, 1024, 512, 256
+P = 128
+PACK = 4
+TILES = V // P
+FLOPS = 2 * 2 * K * S * V
+
+DEGREE = 28
+LOG_PER_BIT = math.log(2.0) / 2.0**23
+PARTS = 2
+
+
+def tile_picked_yhkto_loss_p_kernel(tc, x_words, x_scales, hT, gT, good, lam, offs, out):
+    nc = tc.nc
+    with ExitStack() as ctx:
+        keep = ctx.enter_context(tc.tile_pool(name="keep", bufs=1))
+        psum = ctx.enter_context(tc.psum_pool(name="psum", bufs=1))
+
+        def tiles(name, shape, dtype):
+            return [keep.tile(shape, dtype, name="%s%d" % (name, i), align_bytes=64) for i in range(TILES)]
+
+        offsets = keep.tile([P, S // 16], U16, name="offsets")
+        table_words = keep.tile([P, T], U32, name="table_words", tag="words_then_lam", align_bytes=64)
+        table_scales = keep.tile([P, T], U8, name="table_scales", align_bytes=64)
+
+        nc.gpsimd.memset(table_scales[:].bitcast(I32), 0)
+        nc.sync.dma_start(offsets[:], offs)
+        nc.sync.dma_start(table_words[:].bitcast(I32), x_words[0].rearrange("p n r -> p (n r)").bitcast(I32))
+        for q in range(4):
+            nc.scalar.dma_start(table_scales[32 * q : 32 * q + 4, :].bitcast(I32), x_scales[0, 4 * q : 4 * q + 4, :].bitcast(I32))
+
+        half = DEGREE // 2
+        even_powers = keep.tile([P, half], F32, name="even_powers", tag="h_raw", align_bytes=64)
+        odd_powers = keep.tile([P, half], F32, name="odd_powers", tag="g_raw", align_bytes=64)
+        nc.gpsimd.iota(even_powers[:], [[2, half]], base=-DEGREE, channel_multiplier=0, allow_small_or_imprecise_dtypes=True)
+        nc.gpsimd.iota(odd_powers[:], [[-2, half]], base=DEGREE - 1, channel_multiplier=0, allow_small_or_imprecise_dtypes=True)
+        coeffs = keep.tile([P, half, 2], F32, name="coeffs")
+        nc.vector.reciprocal(coeffs[:, :, 0], even_powers[:])
+        nc.vector.reciprocal(coeffs[:, :, 1], odd_powers[:])
+        horner = tiles("horner", [P, DEGREE + 1], F32)
+        for i in range(TILES):
+            nc.scalar.activation(horner[i][:, :DEGREE], coeffs[:].rearrange("p a b -> p (a b)"), ACT.Copy)
+
+        h_raw = keep.tile([P, PACK, V], F32, name="h_raw", tag="h_raw", align_bytes=64)
+        g_raw = keep.tile([P, PACK, V], F32, name="g_raw", tag="g_raw", align_bytes=64)
+        nc.sync.dma_start(h_raw[:], hT.rearrange("(p j) v -> p j v", j=PACK))
+        nc.sync.dma_start(g_raw[:], gT.rearrange("(p j) v -> p j v", j=PACK))
+
+        picked_scales = keep.tile([P, S], U8, name="picked_scales", align_bytes=64)
+        picked_words = keep.tile([P, S], U32, name="picked_words", align_bytes=64)
+        nc.vector.tensor_copy(picked_scales[:], table_scales[:].indirect(offsets[:]))
+        nc.vector.tensor_copy(picked_words[:], table_words[:].indirect(offsets[:]))
+
+        lam_sb = keep.tile([P, S], F32, name="lam_sb", tag="words_then_lam", align_bytes=64)
+        nc.sync.dma_start(lam_sb[:], lam)
+        half_lam = keep.tile([P, S], F32, name="half_lam", align_bytes=64)
+        nc.gpsimd.tensor_scalar(half_lam[:], lam_sb[:], 0.5, 0.0, ALU.mult, ALU.add)
+
+        def round_and_group(name, raw, copies):
+            grouped = tiles(name + "_grouped", [P, P, PACK], BF16)
+            for i in range(TILES):
+                dst = grouped[i][:].rearrange("p (c e) j -> p c j e", e=4)
+                src = raw[:, :, i * P : (i + 1) * P].rearrange("p j (c e) -> p c j e", e=4)
+                copies[i](dst, src)
+            return grouped
+
+        def product(name, grouped):
+            codes = keep.tile([P, P], U32, name=name + "_codes", align_bytes=64)
+            scales = keep.tile([P, P], U8, name=name + "_scales", align_bytes=64)
+            bank = psum.tile([P, S], F32, name=name + "_bank")
+            nc.vector.quantize_mx(codes[:].bitcast(FP8X4), scales[:], grouped[:].rearrange("p c j -> p (c j)"))
+            nc.tensor.matmul_mx(
+                bank[:],
+                lhsT=codes[:].bitcast(FP8X4),
+                lhsT_scale=scales[:],
+                rhs=picked_words[:].bitcast(FP8X4),
+                rhs_scale=picked_scales[:],
+                start=True,
+                stop=True,
+            )
+            return bank
+
+        def gpsimd_copy(dst, src):
+            nc.gpsimd.tensor_scalar(dst, src, 1.0, 0.0, ALU.mult, ALU.add)
+
+        neg_y = tiles("neg_y", [P, S], F32)
+        neg_z = tiles("neg_z", [P, S], F32)
+        diff = tiles("diff", [P, S], F32)
+        junk = tiles("junk", [P, S], BF16)
+        arg = tiles("arg", [P, S], F32)
+        tanh = tiles("tanh", [P, S], F32)
+        res = tiles("res", [P, S], F32)
+        col = lambda name: tiles(name, [P, 1], F32)
+        neg_max_y, neg_max_z, sum_y, sum_z = col("neg_max_y"), col("neg_max_z"), col("sum_y"), col("sum_z")
+        inv_sum_y, guess_y, known, ratio = col("inv_sum_y"), col("guess_y"), col("known"), col("ratio")
+        inv_guess, rest, abs_sum, shift = col("inv_guess"), col("rest"), col("abs_sum"), col("shift")
+        series = tiles("series", [P, DEGREE + 1], F32)
+
+        h_grouped = round_and_group("h", h_raw, (nc.vector.tensor_copy, nc.scalar.copy))
+        y = [product("y%d" % i, h_grouped[i]) for i in range(TILES)]
+        good_sb = keep.tile([P, S], F32, name="good_sb", tag="h_raw", align_bytes=64)
+        nc.sync.dma_start(good_sb[:], good)
+        g_grouped = round_and_group("g", g_raw, (nc.scalar.copy, nc.scalar.copy))
+
+        z = []
+        for i in range(TILES):
+            nc.vector.tensor_scalar(neg_y[i][:], y[i][:], -1.0, None, ALU.mult, ALU.min, accum_out=neg_max_y[i][:])
+            z.append(product("z%d" % i, g_grouped[i]))
+            nc.scalar.activation(junk[i][:], y[i][:], ACT.Exp, bias=neg_max_y[i][:], accum_out=sum_y[i][:])
+        for i in range(TILES):
+            nc.vector.tensor_scalar(neg_z[i][:], z[i][:], -1.0, None, ALU.mult, ALU.min, accum_out=neg_max_z[i][:])
+            nc.scalar.activation(guess_y[i][:], sum_y[i][:].bitcast(U32), ACT.Copy, scale=LOG_PER_BIT)
+            nc.scalar.activation(junk[i][:], z[i][:], ACT.Exp, bias=neg_max_z[i][:], accum_out=sum_z[i][:])
+        for i in range(TILES):
+            nc.vector.reciprocal(inv_sum_y[i][:], sum_y[i][:])
+            nc.vector.tensor_scalar(known[i][:], neg_max_y[i][:], neg_max_z[i][:], guess_y[i][:], ALU.subtract, ALU.subtract)
+        for i in range(TILES):
+            bits = sum_z[i][:].bitcast(U32)
+            nc.scalar.activation(inv_guess[i][:], bits, ACT.Exp, scale=-LOG_PER_BIT, bias=guess_y[i][:])
+            nc.scalar.activation(ratio[i][:], sum_z[i][:], ACT.Copy, scale=inv_sum_y[i][:])
+            nc.scalar.activation(horner[i][:, DEGREE:], bits, ACT.Identity, scale=LOG_PER_BIT, bias=known[i][:])
+            nc.scalar.activation(rest[i][:], inv_guess[i][:], ACT.Identity, scale=ratio[i][:], bias=-1.0)
+            nc.vector.tensor_tensor_scan(series[i][:], rest[i][:].to_broadcast([P, DEGREE + 1]), horner[i][:], 0.0, ALU.mult, ALU.add)
+            (nc.vector, nc.vector)[i].tensor_tensor(diff[i][:], neg_z[i][:], neg_y[i][:], ALU.subtract)
+        for i in range(TILES):
+            neg_c = series[i][:, DEGREE:]
+            nc.scalar.activation(junk[i][:], diff[i][:], ACT.Abs, bias=neg_c, accum_out=abs_sum[i][:])
+            nc.vector.tensor_scalar(shift[i][:], abs_sum[i][:], -0.3 / S, neg_c, ALU.mult, ALU.add)
+        width = S // PARTS
+        for i in range(TILES):
+            for part in range(PARTS):
+                cols = slice(part * width, (part + 1) * width)
+                nc.vector.scalar_tensor_tensor(arg[i][:, cols], diff[i][:, cols], shift[i][:], good_sb[:, cols], ALU.add, ALU.mult)
+                nc.scalar.activation(tanh[i][:, cols], arg[i][:, cols], ACT.Tanh, scale=-0.75)
+        for i in range(TILES):
+            for part in range(PARTS):
+                cols = slice(part * width, (part + 1) * width)
+                nc.vector.scalar_tensor_tensor(res[i][:, cols], tanh[i][:, cols], 1.0, half_lam[:, cols], ALU.add, ALU.mult)
+                nc.sync.dma_start(out[i * P : (i + 1) * P, cols], res[i][:, cols])

@@ -34,39 +34,42 @@ def tile_picked_yhkto_loss_p_kernel(tc, x_words, x_scales, hT, gT, good, lam, of
             return [keep.tile(shape, dtype, name="%s%d" % (name, i), align_bytes=64) for i in range(TILES)]
 
         offsets = keep.tile([P, S // 16], U16, name="offsets")
-        table_words = keep.tile([P, T], U32, name="table_words", tag="words_then_lam", align_bytes=64)
-        table_scales = keep.tile([P, T], U8, name="table_scales", align_bytes=64)
+        table_words = keep.tile([P, T], U32, name="table_words", tag="words_then_good", align_bytes=64)
+        table_scales = keep.tile([P, T], U8, name="table_scales", tag="scales_then_words", align_bytes=64)
 
-        nc.gpsimd.memset(table_scales[:].bitcast(I32), 0)
+        nc.vector.memset(table_scales[:].bitcast(I32), 0)
         nc.sync.dma_start(offsets[:], offs)
         nc.sync.dma_start(table_words[:].bitcast(I32), x_words[0].rearrange("p n r -> p (n r)").bitcast(I32))
         for q in range(4):
             nc.scalar.dma_start(table_scales[32 * q : 32 * q + 4, :].bitcast(I32), x_scales[0, 4 * q : 4 * q + 4, :].bitcast(I32))
-
-        half = DEGREE // 2
-        even_powers = keep.tile([P, half], F32, name="even_powers", tag="h_raw", align_bytes=64)
-        odd_powers = keep.tile([P, half], F32, name="odd_powers", tag="g_raw", align_bytes=64)
-        nc.gpsimd.iota(even_powers[:], [[2, half]], base=-DEGREE, channel_multiplier=0, allow_small_or_imprecise_dtypes=True)
-        nc.gpsimd.iota(odd_powers[:], [[-2, half]], base=DEGREE - 1, channel_multiplier=0, allow_small_or_imprecise_dtypes=True)
-        coeffs = keep.tile([P, half, 2], F32, name="coeffs")
-        nc.vector.reciprocal(coeffs[:, :, 0], even_powers[:])
-        nc.vector.reciprocal(coeffs[:, :, 1], odd_powers[:])
-        horner = tiles("horner", [P, DEGREE + 1], F32)
-        for i in range(TILES):
-            nc.scalar.activation(horner[i][:, :DEGREE], coeffs[:].rearrange("p a b -> p (a b)"), ACT.Copy)
 
         h_raw = keep.tile([P, PACK, V], F32, name="h_raw", tag="h_raw", align_bytes=64)
         g_raw = keep.tile([P, PACK, V], F32, name="g_raw", tag="g_raw", align_bytes=64)
         nc.sync.dma_start(h_raw[:], hT.rearrange("(p j) v -> p j v", j=PACK))
         nc.sync.dma_start(g_raw[:], gT.rearrange("(p j) v -> p j v", j=PACK))
 
+        half = DEGREE // 2
+        ones = keep.tile([P, half], F32, name="ones")
+        powers = keep.tile([P, half, 2], F32, name="powers", tag="powers_then_lam", align_bytes=64)
+        horner = tiles("horner", [P, DEGREE + 2], F32)
+        rest = tiles("rest", [P, DEGREE + 2], F32)
+        nc.vector.memset(ones[:], 1.0)
+        nc.vector.tensor_tensor_scan(powers[:, :, 0], ones[:], ones[:], -(DEGREE + 2.0), ALU.add, ALU.add)
+        nc.vector.tensor_scalar(powers[:, :, 1], powers[:, :, 0], -1.0, -1.0, ALU.mult, ALU.add)
+        nc.vector.reciprocal(horner[0][:, :DEGREE], powers[:].rearrange("p a b -> p (a b)"))
+        nc.vector.tensor_scalar(rest[1][:, DEGREE + 1 :], ones[:, :1], 0.3 / S, None, ALU.mult)
+        nc.vector.memset(horner[1][:, DEGREE + 1 :], 0.0)
+        nc.scalar.activation(horner[1][:, :DEGREE], horner[0][:, :DEGREE], ACT.Copy)
+
         picked_scales = keep.tile([P, S], U8, name="picked_scales", align_bytes=64)
-        picked_words = keep.tile([P, S], U32, name="picked_words", align_bytes=64)
         nc.vector.tensor_copy(picked_scales[:], table_scales[:].indirect(offsets[:]))
+        picked_words = keep.tile([P, S], U32, name="picked_words", tag="scales_then_words", align_bytes=64)
         nc.vector.tensor_copy(picked_words[:], table_words[:].indirect(offsets[:]))
 
-        lam_sb = keep.tile([P, S], F32, name="lam_sb", tag="words_then_lam", align_bytes=64)
+        lam_sb = keep.tile([P, S], F32, name="lam_sb", tag="powers_then_lam", align_bytes=64)
         nc.sync.dma_start(lam_sb[:], lam)
+        good_sb = keep.tile([P, S], F32, name="good_sb", tag="words_then_good", align_bytes=64)
+        nc.sync.dma_start(good_sb[:], good)
         half_lam = keep.tile([P, S], F32, name="half_lam", align_bytes=64)
         nc.gpsimd.tensor_scalar(half_lam[:], lam_sb[:], 0.5, 0.0, ALU.mult, ALU.add)
 
@@ -78,8 +81,8 @@ def tile_picked_yhkto_loss_p_kernel(tc, x_words, x_scales, hT, gT, good, lam, of
                 copies[i](dst, src)
             return grouped
 
-        def product(name, grouped):
-            codes = keep.tile([P, P], U32, name=name + "_codes", align_bytes=64)
+        def product(name, i, grouped):
+            codes = keep.tile([P, P], U32, name=name + "_codes", tag="codes%d" % i, align_bytes=64)
             scales = keep.tile([P, P], U8, name=name + "_scales", align_bytes=64)
             bank = psum.tile([P, S], F32, name=name + "_bank")
             nc.vector.quantize_mx(codes[:].bitcast(FP8X4), scales[:], grouped[:].rearrange("p c j -> p (c j)"))
@@ -97,7 +100,6 @@ def tile_picked_yhkto_loss_p_kernel(tc, x_words, x_scales, hT, gT, good, lam, of
         def gpsimd_copy(dst, src):
             nc.gpsimd.tensor_scalar(dst, src, 1.0, 0.0, ALU.mult, ALU.add)
 
-        neg_y = tiles("neg_y", [P, S], F32)
         neg_z = tiles("neg_z", [P, S], F32)
         diff = tiles("diff", [P, S], F32)
         junk = tiles("junk", [P, S], BF16)
@@ -107,44 +109,52 @@ def tile_picked_yhkto_loss_p_kernel(tc, x_words, x_scales, hT, gT, good, lam, of
         col = lambda name: tiles(name, [P, 1], F32)
         neg_max_y, neg_max_z, sum_y, sum_z = col("neg_max_y"), col("neg_max_z"), col("sum_y"), col("sum_z")
         inv_sum_y, guess_y, known, ratio = col("inv_sum_y"), col("guess_y"), col("known"), col("ratio")
-        inv_guess, rest, abs_sum, shift = col("inv_guess"), col("rest"), col("abs_sum"), col("shift")
-        series = tiles("series", [P, DEGREE + 1], F32)
+        inv_guess, abs_sum, shift = col("inv_guess"), col("abs_sum"), col("shift")
+        series = tiles("series", [P, DEGREE + 2], F32)
+        reward = keep.tile([P, S], F32, name="reward", align_bytes=64)
 
         h_grouped = round_and_group("h", h_raw, (nc.vector.tensor_copy, nc.scalar.copy))
-        y = [product("y%d" % i, h_grouped[i]) for i in range(TILES)]
-        good_sb = keep.tile([P, S], F32, name="good_sb", tag="h_raw", align_bytes=64)
-        nc.sync.dma_start(good_sb[:], good)
-        g_grouped = round_and_group("g", g_raw, (nc.scalar.copy, nc.scalar.copy))
+        y = [product("y%d" % i, i, h_grouped[i]) for i in range(TILES)]
+        g_grouped = round_and_group("g", g_raw, (nc.scalar.copy, nc.vector.tensor_copy))
 
-        z = []
+        neg_y = [keep.tile([P, S], F32, name="neg_y%d" % i, tag=("h_raw", "g_raw")[i], align_bytes=64) for i in range(TILES)]
+        nc.vector.tensor_scalar(neg_y[0][:], y[0][:], -1.0, None, ALU.mult, ALU.min, accum_out=neg_max_y[0][:])
+        z = [product("z%d" % i, i, g_grouped[i]) for i in range(TILES)]
+        nc.vector.tensor_scalar(neg_y[1][:], y[1][:], -1.0, None, ALU.mult, ALU.min, accum_out=neg_max_y[1][:])
         for i in range(TILES):
-            nc.vector.tensor_scalar(neg_y[i][:], y[i][:], -1.0, None, ALU.mult, ALU.min, accum_out=neg_max_y[i][:])
-            z.append(product("z%d" % i, g_grouped[i]))
             nc.scalar.activation(junk[i][:], y[i][:], ACT.Exp, bias=neg_max_y[i][:], accum_out=sum_y[i][:])
+            nc.scalar.activation(guess_y[i][:], sum_y[i][:].bitcast(U32), ACT.Copy, scale=LOG_PER_BIT)
         for i in range(TILES):
             nc.vector.tensor_scalar(neg_z[i][:], z[i][:], -1.0, None, ALU.mult, ALU.min, accum_out=neg_max_z[i][:])
-            nc.scalar.activation(guess_y[i][:], sum_y[i][:].bitcast(U32), ACT.Copy, scale=LOG_PER_BIT)
             nc.scalar.activation(junk[i][:], z[i][:], ACT.Exp, bias=neg_max_z[i][:], accum_out=sum_z[i][:])
+            nc.scalar.activation(inv_guess[i][:], sum_z[i][:].bitcast(U32), ACT.Exp, scale=-LOG_PER_BIT, bias=guess_y[i][:])
+        nc.gpsimd.tensor_tensor(diff[0][:], neg_z[0][:], neg_y[0][:], ALU.subtract)
         for i in range(TILES):
             nc.vector.reciprocal(inv_sum_y[i][:], sum_y[i][:])
             nc.vector.tensor_scalar(known[i][:], neg_max_y[i][:], neg_max_z[i][:], guess_y[i][:], ALU.subtract, ALU.subtract)
         for i in range(TILES):
-            bits = sum_z[i][:].bitcast(U32)
-            nc.scalar.activation(inv_guess[i][:], bits, ACT.Exp, scale=-LOG_PER_BIT, bias=guess_y[i][:])
-            nc.scalar.activation(ratio[i][:], sum_z[i][:], ACT.Copy, scale=inv_sum_y[i][:])
-            nc.scalar.activation(horner[i][:, DEGREE:], bits, ACT.Identity, scale=LOG_PER_BIT, bias=known[i][:])
-            nc.scalar.activation(rest[i][:], inv_guess[i][:], ACT.Identity, scale=ratio[i][:], bias=-1.0)
-            nc.vector.tensor_tensor_scan(series[i][:], rest[i][:].to_broadcast([P, DEGREE + 1]), horner[i][:], 0.0, ALU.mult, ALU.add)
-            (nc.vector, nc.vector)[i].tensor_tensor(diff[i][:], neg_z[i][:], neg_y[i][:], ALU.subtract)
-        for i in range(TILES):
-            neg_c = series[i][:, DEGREE:]
-            nc.scalar.activation(junk[i][:], diff[i][:], ACT.Abs, bias=neg_c, accum_out=abs_sum[i][:])
-            nc.vector.tensor_scalar(shift[i][:], abs_sum[i][:], -0.3 / S, neg_c, ALU.mult, ALU.add)
+            if i == 0:
+                nc.vector.tensor_scalar(ratio[i][:], sum_z[i][:], inv_sum_y[i][:], None, ALU.mult)
+                nc.vector.tensor_scalar(horner[i][:, DEGREE : DEGREE + 1], sum_z[i][:].bitcast(I32), LOG_PER_BIT, known[i][:], ALU.mult, ALU.add)
+            else:
+                nc.scalar.activation(ratio[i][:], sum_z[i][:], ACT.Copy, scale=inv_sum_y[i][:])
+                nc.scalar.activation(horner[i][:, DEGREE : DEGREE + 1], sum_z[i][:].bitcast(U32), ACT.Identity, scale=LOG_PER_BIT, bias=known[i][:])
+            steps = DEGREE + 1 + i
+            nc.vector.tensor_scalar(rest[i][:, : DEGREE + 1], inv_guess[i][:].to_broadcast([P, DEGREE + 1]), ratio[i][:], -1.0, ALU.mult, ALU.add)
+            nc.vector.tensor_tensor_scan(series[i][:, :steps], rest[i][:, :steps], horner[i][:, :steps], 0.0, ALU.mult, ALU.add)
+            if i == 0:
+                nc.vector.tensor_tensor(diff[1][:], y[1][:], neg_z[1][:], ALU.add)
+        neg_c = [series[i][:, DEGREE : DEGREE + 1] for i in range(TILES)]
+        nc.scalar.activation(junk[0][:], diff[0][:], ACT.Abs, bias=neg_c[0], accum_out=abs_sum[0][:])
+        nc.scalar.activation(junk[1][:], diff[1][:], ACT.Abs, scale=0.3 / S, bias=series[1][:, DEGREE + 1 :], accum_out=abs_sum[1][:])
+        nc.vector.tensor_scalar(shift[0][:], abs_sum[0][:], -0.3 / S, neg_c[0], ALU.mult, ALU.add)
+        nc.vector.tensor_scalar(reward[:], diff[1][:], neg_c[1], None, ALU.add)
+        first = ((diff[0], shift[0], ALU.add), (reward, abs_sum[1], ALU.subtract))
         width = S // PARTS
         for i in range(TILES):
             for part in range(PARTS):
                 cols = slice(part * width, (part + 1) * width)
-                nc.vector.scalar_tensor_tensor(arg[i][:, cols], diff[i][:, cols], shift[i][:], good_sb[:, cols], ALU.add, ALU.mult)
+                nc.vector.scalar_tensor_tensor(arg[i][:, cols], first[i][0][:, cols], first[i][1][:], good_sb[:, cols], first[i][2], ALU.mult)
                 nc.scalar.activation(tanh[i][:, cols], arg[i][:, cols], ACT.Tanh, scale=-0.75)
         for i in range(TILES):
             for part in range(PARTS):

@@ -34,44 +34,44 @@ def tile_picked_yhkto_loss_p_kernel(tc, x_words, x_scales, hT, gT, good, lam, of
             return [keep.tile(shape, dtype, name="%s%d" % (name, i), align_bytes=64) for i in range(TILES)]
 
         offsets = keep.tile([P, S // 16], U16, name="offsets")
-        table_words = keep.tile([P, T], U32, name="table_words", tag="words_then_good", align_bytes=64)
-        table_scales = keep.tile([P, T], U8, name="table_scales", tag="scales_then_words", align_bytes=64)
-
-        nc.vector.memset(table_scales[:].bitcast(I32), 0)
         nc.sync.dma_start(offsets[:], offs)
+        table_words = keep.tile([P, T], U32, name="table_words", tag="words_then_good", align_bytes=64)
         nc.sync.dma_start(table_words[:].bitcast(I32), x_words[0].rearrange("p n r -> p (n r)").bitcast(I32))
+        table_scales = keep.tile([P, T], U8, name="table_scales", tag="scales_then_lam", align_bytes=64)
+        nc.vector.memset(table_scales[:].bitcast(I32), 0)
         for q in range(4):
-            nc.scalar.dma_start(table_scales[32 * q : 32 * q + 4, :].bitcast(I32), x_scales[0, 4 * q : 4 * q + 4, :].bitcast(I32))
+            nc.sync.dma_start(table_scales[32 * q : 32 * q + 4, :].bitcast(I32), x_scales[0, 4 * q : 4 * q + 4, :].bitcast(I32))
+
+        half = DEGREE // 2
+        ones = keep.tile([P, half], F32, name="ones", tag="h_raw", align_bytes=64)
+        even_powers = keep.tile([P, half], F32, name="even_powers", tag="g_raw", align_bytes=64)
+        odd_powers = keep.tile([P, half], F32, name="odd_powers")
+        horner = tiles("horner", [P, DEGREE + 2], F32)
+        rest = tiles("rest", [P, DEGREE + 2], F32)
+        nc.vector.memset(ones[:], 1.0)
+        nc.vector.memset(horner[1][:, DEGREE + 1 :], 0.0)
+        nc.vector.tensor_scalar(rest[1][:, DEGREE + 1 :], ones[:, :1], 0.3 / S, None, ALU.mult)
+        nc.vector.tensor_tensor_scan(even_powers[:], ones[:], ones[:], -(DEGREE + 2.0), ALU.add, ALU.add)
+        nc.vector.tensor_scalar(odd_powers[:], even_powers[:], -1.0, -1.0, ALU.mult, ALU.add)
+        nc.vector.reciprocal(horner[0][:, 0:DEGREE:2], even_powers[:])
+        nc.vector.reciprocal(horner[0][:, 1:DEGREE:2], odd_powers[:])
+        nc.scalar.activation(horner[1][:, :DEGREE], horner[0][:, :DEGREE], ACT.Copy)
 
         h_raw = keep.tile([P, PACK, V], F32, name="h_raw", tag="h_raw", align_bytes=64)
         g_raw = keep.tile([P, PACK, V], F32, name="g_raw", tag="g_raw", align_bytes=64)
         nc.sync.dma_start(h_raw[:], hT.rearrange("(p j) v -> p j v", j=PACK))
         nc.sync.dma_start(g_raw[:], gT.rearrange("(p j) v -> p j v", j=PACK))
 
-        half = DEGREE // 2
-        ones = keep.tile([P, half], F32, name="ones")
-        powers = keep.tile([P, half, 2], F32, name="powers", tag="powers_then_lam", align_bytes=64)
-        horner = tiles("horner", [P, DEGREE + 2], F32)
-        rest = tiles("rest", [P, DEGREE + 2], F32)
-        nc.vector.memset(ones[:], 1.0)
-        nc.vector.tensor_tensor_scan(powers[:, :, 0], ones[:], ones[:], -(DEGREE + 2.0), ALU.add, ALU.add)
-        nc.vector.tensor_scalar(powers[:, :, 1], powers[:, :, 0], -1.0, -1.0, ALU.mult, ALU.add)
-        nc.vector.reciprocal(horner[0][:, :DEGREE], powers[:].rearrange("p a b -> p (a b)"))
-        nc.vector.tensor_scalar(rest[1][:, DEGREE + 1 :], ones[:, :1], 0.3 / S, None, ALU.mult)
-        nc.vector.memset(horner[1][:, DEGREE + 1 :], 0.0)
-        nc.scalar.activation(horner[1][:, :DEGREE], horner[0][:, :DEGREE], ACT.Copy)
-
         picked_scales = keep.tile([P, S], U8, name="picked_scales", align_bytes=64)
-        nc.vector.tensor_copy(picked_scales[:], table_scales[:].indirect(offsets[:]))
-        picked_words = keep.tile([P, S], U32, name="picked_words", tag="scales_then_words", align_bytes=64)
+        picked_words = keep.tile([P, S], U32, name="picked_words", align_bytes=64)
         nc.vector.tensor_copy(picked_words[:], table_words[:].indirect(offsets[:]))
+        nc.vector.tensor_copy(picked_scales[:], table_scales[:].indirect(offsets[:]))
 
-        lam_sb = keep.tile([P, S], F32, name="lam_sb", tag="powers_then_lam", align_bytes=64)
+        lam_sb = keep.tile([P, S], F32, name="lam_sb", tag="words_then_good", align_bytes=64)
         nc.sync.dma_start(lam_sb[:], lam)
-        good_sb = keep.tile([P, S], F32, name="good_sb", tag="words_then_good", align_bytes=64)
+        good_sb = keep.tile([P, S], F32, name="good_sb", tag="scales_then_lam", align_bytes=64)
         nc.sync.dma_start(good_sb[:], good)
         half_lam = keep.tile([P, S], F32, name="half_lam", align_bytes=64)
-        nc.gpsimd.tensor_scalar(half_lam[:], lam_sb[:], 0.5, 0.0, ALU.mult, ALU.add)
 
         def round_and_group(name, raw, copies):
             grouped = tiles(name + "_grouped", [P, P, PACK], BF16)
@@ -82,7 +82,7 @@ def tile_picked_yhkto_loss_p_kernel(tc, x_words, x_scales, hT, gT, good, lam, of
             return grouped
 
         def product(name, i, grouped):
-            codes = keep.tile([P, P], U32, name=name + "_codes", tag="codes%d" % i, align_bytes=64)
+            codes = keep.tile([P, P], U32, name=name + "_codes", align_bytes=64)
             scales = keep.tile([P, P], U8, name=name + "_scales", align_bytes=64)
             bank = psum.tile([P, S], F32, name=name + "_bank")
             nc.vector.quantize_mx(codes[:].bitcast(FP8X4), scales[:], grouped[:].rearrange("p c j -> p (c j)"))
@@ -113,22 +113,26 @@ def tile_picked_yhkto_loss_p_kernel(tc, x_words, x_scales, hT, gT, good, lam, of
         series = tiles("series", [P, DEGREE + 2], F32)
         reward = keep.tile([P, S], F32, name="reward", align_bytes=64)
 
-        h_grouped = round_and_group("h", h_raw, (nc.vector.tensor_copy, nc.scalar.copy))
+        h_grouped = round_and_group("h", h_raw, (nc.scalar.copy, nc.scalar.copy))
         y = [product("y%d" % i, i, h_grouped[i]) for i in range(TILES)]
-        g_grouped = round_and_group("g", g_raw, (nc.scalar.copy, nc.vector.tensor_copy))
+        g_grouped = round_and_group("g", g_raw, (nc.vector.tensor_copy, nc.scalar.copy))
 
-        neg_y = [keep.tile([P, S], F32, name="neg_y%d" % i, tag=("h_raw", "g_raw")[i], align_bytes=64) for i in range(TILES)]
-        nc.vector.tensor_scalar(neg_y[0][:], y[0][:], -1.0, None, ALU.mult, ALU.min, accum_out=neg_max_y[0][:])
-        z = [product("z%d" % i, i, g_grouped[i]) for i in range(TILES)]
-        nc.vector.tensor_scalar(neg_y[1][:], y[1][:], -1.0, None, ALU.mult, ALU.min, accum_out=neg_max_y[1][:])
+        nc.scalar.activation(half_lam[:], lam_sb[:], ACT.Copy, scale=0.5)
+        neg_y = [keep.tile([P, S], F32, name="neg_y%d" % i, tag=("g_raw", "h_raw")[i], align_bytes=64) for i in range(TILES)]
+        z = [product("z0", 0, g_grouped[0])]
         for i in range(TILES):
+            nc.vector.tensor_scalar(neg_y[i][:], y[i][:], -1.0, None, ALU.mult, ALU.min, accum_out=neg_max_y[i][:])
+            if i == 0:
+                z.append(product("z1", 1, g_grouped[1]))
+            if i == 0:
+                nc.vector.tensor_scalar(neg_z[i][:], z[i][:], -1.0, None, ALU.mult, ALU.min, accum_out=neg_max_z[i][:])
+                nc.gpsimd.tensor_tensor(diff[i][:], neg_z[i][:], neg_y[i][:], ALU.subtract)
+            else:
+                nc.vector.tensor_reduce(neg_max_z[i][:], z[i][:], mybir.AxisListType.X, ALU.max, negate=True)
             nc.scalar.activation(junk[i][:], y[i][:], ACT.Exp, bias=neg_max_y[i][:], accum_out=sum_y[i][:])
-            nc.scalar.activation(guess_y[i][:], sum_y[i][:].bitcast(U32), ACT.Copy, scale=LOG_PER_BIT)
-        for i in range(TILES):
-            nc.vector.tensor_scalar(neg_z[i][:], z[i][:], -1.0, None, ALU.mult, ALU.min, accum_out=neg_max_z[i][:])
             nc.scalar.activation(junk[i][:], z[i][:], ACT.Exp, bias=neg_max_z[i][:], accum_out=sum_z[i][:])
+            nc.scalar.activation(guess_y[i][:], sum_y[i][:].bitcast(U32), ACT.Copy, scale=LOG_PER_BIT)
             nc.scalar.activation(inv_guess[i][:], sum_z[i][:].bitcast(U32), ACT.Exp, scale=-LOG_PER_BIT, bias=guess_y[i][:])
-        nc.gpsimd.tensor_tensor(diff[0][:], neg_z[0][:], neg_y[0][:], ALU.subtract)
         for i in range(TILES):
             nc.vector.reciprocal(inv_sum_y[i][:], sum_y[i][:])
             nc.vector.tensor_scalar(known[i][:], neg_max_y[i][:], neg_max_z[i][:], guess_y[i][:], ALU.subtract, ALU.subtract)
@@ -143,7 +147,7 @@ def tile_picked_yhkto_loss_p_kernel(tc, x_words, x_scales, hT, gT, good, lam, of
             nc.vector.tensor_scalar(rest[i][:, : DEGREE + 1], inv_guess[i][:].to_broadcast([P, DEGREE + 1]), ratio[i][:], -1.0, ALU.mult, ALU.add)
             nc.vector.tensor_tensor_scan(series[i][:, :steps], rest[i][:, :steps], horner[i][:, :steps], 0.0, ALU.mult, ALU.add)
             if i == 0:
-                nc.vector.tensor_tensor(diff[1][:], y[1][:], neg_z[1][:], ALU.add)
+                nc.vector.scalar_tensor_tensor(diff[1][:], z[1][:], -1.0, neg_y[1][:], ALU.mult, ALU.subtract)
         neg_c = [series[i][:, DEGREE : DEGREE + 1] for i in range(TILES)]
         nc.scalar.activation(junk[0][:], diff[0][:], ACT.Abs, bias=neg_c[0], accum_out=abs_sum[0][:])
         nc.scalar.activation(junk[1][:], diff[1][:], ACT.Abs, scale=0.3 / S, bias=series[1][:, DEGREE + 1 :], accum_out=abs_sum[1][:])

@@ -16,11 +16,13 @@ ALU = mybir.AluOpType
 K, T, S, V = 512, 1024, 512, 256
 P = 128
 PACK = 4
+QUADRANTS = 4
 TILES = V // P
 FLOPS = 2 * 2 * K * S * V
 
-DEGREE = 28
 LOG_PER_BIT = math.log(2.0) / 2.0**23
+DEGREE = 28
+MEAN_SHARE = 0.3 / S
 PARTS = 2
 
 
@@ -35,11 +37,11 @@ def tile_picked_yhkto_loss_p_kernel(tc, x_words, x_scales, hT, gT, good, lam, of
 
         offsets = keep.tile([P, S // 16], U16, name="offsets")
         nc.sync.dma_start(offsets[:], offs)
-        table_words = keep.tile([P, T], U32, name="table_words", tag="words_then_good", align_bytes=64)
+        table_words = keep.tile([P, T], U32, name="table_words", tag="words_then_lam", align_bytes=64)
         nc.sync.dma_start(table_words[:].bitcast(I32), x_words[0].rearrange("p n r -> p (n r)").bitcast(I32))
-        table_scales = keep.tile([P, T], U8, name="table_scales", tag="scales_then_lam", align_bytes=64)
+        table_scales = keep.tile([P, T], U8, name="table_scales", tag="scales_then_good", align_bytes=64)
         nc.vector.memset(table_scales[:].bitcast(I32), 0)
-        for q in range(4):
+        for q in range(QUADRANTS):
             nc.sync.dma_start(table_scales[32 * q : 32 * q + 4, :].bitcast(I32), x_scales[0, 4 * q : 4 * q + 4, :].bitcast(I32))
 
         half = DEGREE // 2
@@ -50,7 +52,7 @@ def tile_picked_yhkto_loss_p_kernel(tc, x_words, x_scales, hT, gT, good, lam, of
         rest = tiles("rest", [P, DEGREE + 2], F32)
         nc.vector.memset(ones[:], 1.0)
         nc.vector.memset(horner[1][:, DEGREE + 1 :], 0.0)
-        nc.vector.tensor_scalar(rest[1][:, DEGREE + 1 :], ones[:, :1], 0.3 / S, None, ALU.mult)
+        nc.vector.tensor_scalar(rest[1][:, DEGREE + 1 :], ones[:, :1], MEAN_SHARE, None, ALU.mult)
         nc.vector.tensor_tensor_scan(even_powers[:], ones[:], ones[:], -(DEGREE + 2.0), ALU.add, ALU.add)
         nc.vector.tensor_scalar(odd_powers[:], even_powers[:], -1.0, -1.0, ALU.mult, ALU.add)
         nc.vector.reciprocal(horner[0][:, 0:DEGREE:2], even_powers[:])
@@ -67,22 +69,25 @@ def tile_picked_yhkto_loss_p_kernel(tc, x_words, x_scales, hT, gT, good, lam, of
         nc.vector.tensor_copy(picked_words[:], table_words[:].indirect(offsets[:]))
         nc.vector.tensor_copy(picked_scales[:], table_scales[:].indirect(offsets[:]))
 
-        lam_sb = keep.tile([P, S], F32, name="lam_sb", tag="words_then_good", align_bytes=64)
+        lam_sb = keep.tile([P, S], F32, name="lam_sb", tag="words_then_lam", align_bytes=64)
         nc.sync.dma_start(lam_sb[:], lam)
-        good_sb = keep.tile([P, S], F32, name="good_sb", tag="scales_then_lam", align_bytes=64)
+        good_sb = keep.tile([P, S], F32, name="good_sb", tag="scales_then_good", align_bytes=64)
         nc.sync.dma_start(good_sb[:], good)
         half_lam = keep.tile([P, S], F32, name="half_lam", align_bytes=64)
 
         def round_and_group(name, raw, copies):
-            grouped = tiles(name + "_grouped", [P, P, PACK], BF16)
+            grouped = []
+            for i in range(TILES):
+                tag = "%s_grouped%d" % (name, i)
+                grouped.append(keep.tile([P, P, PACK], BF16, name=tag, tag=tag, align_bytes=64))
             for i in range(TILES):
                 dst = grouped[i][:].rearrange("p (c e) j -> p c j e", e=4)
                 src = raw[:, :, i * P : (i + 1) * P].rearrange("p j (c e) -> p c j e", e=4)
                 copies[i](dst, src)
             return grouped
 
-        def product(name, i, grouped):
-            codes = keep.tile([P, P], U32, name=name + "_codes", align_bytes=64)
+        def product(name, codes_tag, grouped):
+            codes = keep.tile([P, P], U32, name=name + "_codes", tag=codes_tag, align_bytes=64)
             scales = keep.tile([P, P], U8, name=name + "_scales", align_bytes=64)
             bank = psum.tile([P, S], F32, name=name + "_bank")
             nc.vector.quantize_mx(codes[:].bitcast(FP8X4), scales[:], grouped[:].rearrange("p c j -> p (c j)"))
@@ -97,68 +102,73 @@ def tile_picked_yhkto_loss_p_kernel(tc, x_words, x_scales, hT, gT, good, lam, of
             )
             return bank
 
-        def gpsimd_copy(dst, src):
-            nc.gpsimd.tensor_scalar(dst, src, 1.0, 0.0, ALU.mult, ALU.add)
+        def columns(name):
+            return tiles(name, [P, 1], F32)
 
-        neg_z = tiles("neg_z", [P, S], F32)
+        neg_z0 = keep.tile([P, S], F32, name="neg_z0", align_bytes=64)
         diff = tiles("diff", [P, S], F32)
-        junk = tiles("junk", [P, S], BF16)
+        summed = tiles("summed", [P, S], BF16)
         arg = tiles("arg", [P, S], F32)
         tanh = tiles("tanh", [P, S], F32)
         res = tiles("res", [P, S], F32)
-        col = lambda name: tiles(name, [P, 1], F32)
-        neg_max_y, neg_max_z, sum_y, sum_z = col("neg_max_y"), col("neg_max_z"), col("sum_y"), col("sum_z")
-        inv_sum_y, guess_y, known, ratio = col("inv_sum_y"), col("guess_y"), col("known"), col("ratio")
-        inv_guess, abs_sum, shift = col("inv_guess"), col("abs_sum"), col("shift")
+        neg_max_y, neg_max_z, sum_y, sum_z = columns("neg_max_y"), columns("neg_max_z"), columns("sum_y"), columns("sum_z")
+        inv_sum_y, guess_y, known, ratio = columns("inv_sum_y"), columns("guess_y"), columns("known"), columns("ratio")
+        inv_guess, abs_sum = columns("inv_guess"), columns("abs_sum")
+        shift0 = keep.tile([P, 1], F32, name="shift0", align_bytes=64)
         series = tiles("series", [P, DEGREE + 2], F32)
-        reward = keep.tile([P, S], F32, name="reward", align_bytes=64)
+        reward1 = keep.tile([P, S], F32, name="reward1", align_bytes=64)
 
         h_grouped = round_and_group("h", h_raw, (nc.scalar.copy, nc.scalar.copy))
-        y = [product("y%d" % i, i, h_grouped[i]) for i in range(TILES)]
+        y = [product("y0", "y0_codes", h_grouped[0])]
         g_grouped = round_and_group("g", g_raw, (nc.vector.tensor_copy, nc.scalar.copy))
-
         nc.scalar.activation(half_lam[:], lam_sb[:], ACT.Copy, scale=0.5)
-        neg_y = [keep.tile([P, S], F32, name="neg_y%d" % i, tag=("g_raw", "h_raw")[i], align_bytes=64) for i in range(TILES)]
-        z = [product("z0", 0, g_grouped[0])]
+        z = [product("z0", "z0_codes", g_grouped[0])]
+        neg_y = [keep.tile([P, S], F32, name="neg_y%d" % i, tag=("g_grouped0", "h_raw")[i], align_bytes=64) for i in range(TILES)]
+
         for i in range(TILES):
             nc.vector.tensor_scalar(neg_y[i][:], y[i][:], -1.0, None, ALU.mult, ALU.min, accum_out=neg_max_y[i][:])
             if i == 0:
-                z.append(product("z1", 1, g_grouped[1]))
-            if i == 0:
-                nc.vector.tensor_scalar(neg_z[i][:], z[i][:], -1.0, None, ALU.mult, ALU.min, accum_out=neg_max_z[i][:])
-                nc.gpsimd.tensor_tensor(diff[i][:], neg_z[i][:], neg_y[i][:], ALU.subtract)
+                y.append(product("y1", "g_raw", h_grouped[1]))
+                z.append(product("z1", "z1_codes", g_grouped[1]))
+                nc.vector.tensor_scalar(neg_z0[:], z[0][:], -1.0, None, ALU.mult, ALU.min, accum_out=neg_max_z[0][:])
+                nc.gpsimd.tensor_tensor(diff[0][:], neg_z0[:], neg_y[0][:], ALU.subtract)
             else:
-                nc.vector.tensor_reduce(neg_max_z[i][:], z[i][:], mybir.AxisListType.X, ALU.max, negate=True)
-            nc.scalar.activation(junk[i][:], y[i][:], ACT.Exp, bias=neg_max_y[i][:], accum_out=sum_y[i][:])
-            nc.scalar.activation(junk[i][:], z[i][:], ACT.Exp, bias=neg_max_z[i][:], accum_out=sum_z[i][:])
+                nc.vector.tensor_reduce(neg_max_z[1][:], z[1][:], mybir.AxisListType.X, ALU.max, negate=True)
+            nc.scalar.activation(summed[i][:], y[i][:], ACT.Exp, bias=neg_max_y[i][:], accum_out=sum_y[i][:])
+            nc.scalar.activation(summed[i][:], z[i][:], ACT.Exp, bias=neg_max_z[i][:], accum_out=sum_z[i][:])
             nc.scalar.activation(guess_y[i][:], sum_y[i][:].bitcast(U32), ACT.Copy, scale=LOG_PER_BIT)
             nc.scalar.activation(inv_guess[i][:], sum_z[i][:].bitcast(U32), ACT.Exp, scale=-LOG_PER_BIT, bias=guess_y[i][:])
         for i in range(TILES):
             nc.vector.reciprocal(inv_sum_y[i][:], sum_y[i][:])
             nc.vector.tensor_scalar(known[i][:], neg_max_y[i][:], neg_max_z[i][:], guess_y[i][:], ALU.subtract, ALU.subtract)
+
         for i in range(TILES):
+            added = horner[i][:, DEGREE : DEGREE + 1]
             if i == 0:
-                nc.vector.tensor_scalar(ratio[i][:], sum_z[i][:], inv_sum_y[i][:], None, ALU.mult)
-                nc.vector.tensor_scalar(horner[i][:, DEGREE : DEGREE + 1], sum_z[i][:].bitcast(I32), LOG_PER_BIT, known[i][:], ALU.mult, ALU.add)
+                nc.vector.tensor_scalar(ratio[0][:], sum_z[0][:], inv_sum_y[0][:], None, ALU.mult)
+                nc.vector.tensor_scalar(added, sum_z[0][:].bitcast(I32), LOG_PER_BIT, known[0][:], ALU.mult, ALU.add)
             else:
-                nc.scalar.activation(ratio[i][:], sum_z[i][:], ACT.Copy, scale=inv_sum_y[i][:])
-                nc.scalar.activation(horner[i][:, DEGREE : DEGREE + 1], sum_z[i][:].bitcast(U32), ACT.Identity, scale=LOG_PER_BIT, bias=known[i][:])
+                nc.scalar.activation(ratio[1][:], sum_z[1][:], ACT.Copy, scale=inv_sum_y[1][:])
+                nc.scalar.activation(added, sum_z[1][:].bitcast(U32), ACT.Identity, scale=LOG_PER_BIT, bias=known[1][:])
             steps = DEGREE + 1 + i
             nc.vector.tensor_scalar(rest[i][:, : DEGREE + 1], inv_guess[i][:].to_broadcast([P, DEGREE + 1]), ratio[i][:], -1.0, ALU.mult, ALU.add)
             nc.vector.tensor_tensor_scan(series[i][:, :steps], rest[i][:, :steps], horner[i][:, :steps], 0.0, ALU.mult, ALU.add)
             if i == 0:
                 nc.vector.scalar_tensor_tensor(diff[1][:], z[1][:], -1.0, neg_y[1][:], ALU.mult, ALU.subtract)
-        neg_c = [series[i][:, DEGREE : DEGREE + 1] for i in range(TILES)]
-        nc.scalar.activation(junk[0][:], diff[0][:], ACT.Abs, bias=neg_c[0], accum_out=abs_sum[0][:])
-        nc.scalar.activation(junk[1][:], diff[1][:], ACT.Abs, scale=0.3 / S, bias=series[1][:, DEGREE + 1 :], accum_out=abs_sum[1][:])
-        nc.vector.tensor_scalar(shift[0][:], abs_sum[0][:], -0.3 / S, neg_c[0], ALU.mult, ALU.add)
-        nc.vector.tensor_scalar(reward[:], diff[1][:], neg_c[1], None, ALU.add)
-        first = ((diff[0], shift[0], ALU.add), (reward, abs_sum[1], ALU.subtract))
+        offset = [series[i][:, DEGREE : DEGREE + 1] for i in range(TILES)]
+
+        nc.scalar.activation(summed[0][:], diff[0][:], ACT.Abs, bias=offset[0], accum_out=abs_sum[0][:])
+        nc.scalar.activation(summed[1][:], diff[1][:], ACT.Abs, scale=MEAN_SHARE, bias=series[1][:, DEGREE + 1 :], accum_out=abs_sum[1][:])
+        nc.vector.tensor_scalar(shift0[:], abs_sum[0][:], -MEAN_SHARE, offset[0], ALU.mult, ALU.add)
+        nc.vector.tensor_scalar(reward1[:], diff[1][:], offset[1], None, ALU.add)
+        centred = ((diff[0], ALU.add, shift0), (reward1, ALU.subtract, abs_sum[1]))
+
         width = S // PARTS
         for i in range(TILES):
+            values, op, row_term = centred[i]
             for part in range(PARTS):
                 cols = slice(part * width, (part + 1) * width)
-                nc.vector.scalar_tensor_tensor(arg[i][:, cols], first[i][0][:, cols], first[i][1][:], good_sb[:, cols], first[i][2], ALU.mult)
+                nc.vector.scalar_tensor_tensor(arg[i][:, cols], values[:, cols], row_term[:], good_sb[:, cols], op, ALU.mult)
                 nc.scalar.activation(tanh[i][:, cols], arg[i][:, cols], ACT.Tanh, scale=-0.75)
         for i in range(TILES):
             for part in range(PARTS):

import math
from contextlib import ExitStack

import concourse.mybir as mybir

F32 = mybir.dt.float32
BF16 = mybir.dt.bfloat16
I32 = mybir.dt.int32
U32 = mybir.dt.uint32
U16 = mybir.dt.uint16
U8 = mybir.dt.uint8
FP8X4 = mybir.dt.float8_e4m3fn_x4
ACT = mybir.ActivationFunctionType
ALU = mybir.AluOpType

K, T, S, V = 512, 1024, 512, 256
P = 128
PACK = 4
QUADRANTS = 4
TILES = V // P
FLOPS = 2 * 2 * K * S * V

LOG_PER_BIT = math.log(2.0) / 2.0**23
DEGREE = 28
MEAN_SHARE = 0.3 / S
PARTS = 2


def tile_picked_yhkto_loss_p_kernel(tc, x_words, x_scales, hT, gT, good, lam, offs, out):
    nc = tc.nc
    with ExitStack() as ctx:
        keep = ctx.enter_context(tc.tile_pool(name="keep", bufs=1))
        psum = ctx.enter_context(tc.psum_pool(name="psum", bufs=1))

        def tiles(name, shape, dtype):
            return [keep.tile(shape, dtype, name="%s%d" % (name, i), align_bytes=64) for i in range(TILES)]

        offsets = keep.tile([P, S // 16], U16, name="offsets")
        nc.sync.dma_start(offsets[:], offs)
        table_words = keep.tile([P, T], U32, name="table_words", tag="words_then_lam", align_bytes=64)
        nc.sync.dma_start(table_words[:].bitcast(I32), x_words[0].rearrange("p n r -> p (n r)").bitcast(I32))
        table_scales = keep.tile([P, T], U8, name="table_scales", tag="scales_then_good", align_bytes=64)
        nc.vector.memset(table_scales[:].bitcast(I32), 0)
        for q in range(QUADRANTS):
            nc.sync.dma_start(table_scales[32 * q : 32 * q + 4, :].bitcast(I32), x_scales[0, 4 * q : 4 * q + 4, :].bitcast(I32))

        half = DEGREE // 2
        ones = keep.tile([P, half], F32, name="ones", tag="h_raw", align_bytes=64)
        even_powers = keep.tile([P, half], F32, name="even_powers", tag="g_raw", align_bytes=64)
        odd_powers = keep.tile([P, half], F32, name="odd_powers")
        horner = tiles("horner", [P, DEGREE + 2], F32)
        rest = tiles("rest", [P, DEGREE + 2], F32)
        nc.vector.memset(ones[:], 1.0)
        nc.vector.memset(horner[1][:, DEGREE + 1 :], 0.0)
        nc.vector.tensor_scalar(rest[1][:, DEGREE + 1 :], ones[:, :1], MEAN_SHARE, None, ALU.mult)
        nc.vector.tensor_tensor_scan(even_powers[:], ones[:], ones[:], -(DEGREE + 2.0), ALU.add, ALU.add)
        nc.vector.tensor_scalar(odd_powers[:], even_powers[:], -1.0, -1.0, ALU.mult, ALU.add)
        nc.vector.reciprocal(horner[0][:, 0:DEGREE:2], even_powers[:])
        nc.vector.reciprocal(horner[0][:, 1:DEGREE:2], odd_powers[:])
        nc.scalar.activation(horner[1][:, :DEGREE], horner[0][:, :DEGREE], ACT.Copy)

        h_raw = keep.tile([P, PACK, V], F32, name="h_raw", tag="h_raw", align_bytes=64)
        g_raw = keep.tile([P, PACK, V], F32, name="g_raw", tag="g_raw", align_bytes=64)
        nc.sync.dma_start(h_raw[:], hT.rearrange("(p j) v -> p j v", j=PACK))
        nc.sync.dma_start(g_raw[:], gT.rearrange("(p j) v -> p j v", j=PACK))

        picked_scales = keep.tile([P, S], U8, name="picked_scales", align_bytes=64)
        picked_words = keep.tile([P, S], U32, name="picked_words", align_bytes=64)
        nc.vector.tensor_copy(picked_words[:], table_words[:].indirect(offsets[:]))
        nc.vector.tensor_copy(picked_scales[:], table_scales[:].indirect(offsets[:]))

        lam_sb = keep.tile([P, S], F32, name="lam_sb", tag="words_then_lam", align_bytes=64)
        nc.sync.dma_start(lam_sb[:], lam)
        good_sb = keep.tile([P, S], F32, name="good_sb", tag="scales_then_good", align_bytes=64)
        nc.sync.dma_start(good_sb[:], good)
        half_lam = keep.tile([P, S], F32, name="half_lam", align_bytes=64)

        def round_and_group(name, raw, copies):
            grouped = []
            for i in range(TILES):
                tag = "%s_grouped%d" % (name, i)
                grouped.append(keep.tile([P, P, PACK], BF16, name=tag, tag=tag, align_bytes=64))
            for i in range(TILES):
                dst = grouped[i][:].rearrange("p (c e) j -> p c j e", e=4)
                src = raw[:, :, i * P : (i + 1) * P].rearrange("p j (c e) -> p c j e", e=4)
                copies[i](dst, src)
            return grouped

        def product(name, codes_tag, grouped):
            codes = keep.tile([P, P], U32, name=name + "_codes", tag=codes_tag, align_bytes=64)
            scales = keep.tile([P, P], U8, name=name + "_scales", align_bytes=64)
            bank = psum.tile([P, S], F32, name=name + "_bank")
            nc.vector.quantize_mx(codes[:].bitcast(FP8X4), scales[:], grouped[:].rearrange("p c j -> p (c j)"))
            nc.tensor.matmul_mx(
                bank[:],
                lhsT=codes[:].bitcast(FP8X4),
                lhsT_scale=scales[:],
                rhs=picked_words[:].bitcast(FP8X4),
                rhs_scale=picked_scales[:],
                start=True,
                stop=True,
            )
            return bank

        def columns(name):
            return tiles(name, [P, 1], F32)

        neg_z0 = keep.tile([P, S], F32, name="neg_z0", align_bytes=64)
        diff = tiles("diff", [P, S], F32)
        summed = tiles("summed", [P, S], BF16)
        arg = tiles("arg", [P, S], F32)
        tanh = tiles("tanh", [P, S], F32)
        res = tiles("res", [P, S], F32)
        neg_max_y, neg_max_z, sum_y, sum_z = columns("neg_max_y"), columns("neg_max_z"), columns("sum_y"), columns("sum_z")
        inv_sum_y, guess_y, known, ratio = columns("inv_sum_y"), columns("guess_y"), columns("known"), columns("ratio")
        inv_guess, abs_sum = columns("inv_guess"), columns("abs_sum")
        shift0 = keep.tile([P, 1], F32, name="shift0", align_bytes=64)
        series = tiles("series", [P, DEGREE + 2], F32)
        reward1 = keep.tile([P, S], F32, name="reward1", align_bytes=64)

        h_grouped = round_and_group("h", h_raw, (nc.scalar.copy, nc.scalar.copy))
        y = [product("y0", "y0_codes", h_grouped[0])]
        g_grouped = round_and_group("g", g_raw, (nc.vector.tensor_copy, nc.scalar.copy))
        nc.scalar.activation(half_lam[:], lam_sb[:], ACT.Copy, scale=0.5)
        z = [product("z0", "z0_codes", g_grouped[0])]
        neg_y = [keep.tile([P, S], F32, name="neg_y%d" % i, tag=("g_grouped0", "h_raw")[i], align_bytes=64) for i in range(TILES)]

        for i in range(TILES):
            nc.vector.tensor_scalar(neg_y[i][:], y[i][:], -1.0, None, ALU.mult, ALU.min, accum_out=neg_max_y[i][:])
            if i == 0:
                y.append(product("y1", "g_raw", h_grouped[1]))
                z.append(product("z1", "z1_codes", g_grouped[1]))
                nc.vector.tensor_scalar(neg_z0[:], z[0][:], -1.0, None, ALU.mult, ALU.min, accum_out=neg_max_z[0][:])
                nc.gpsimd.tensor_tensor(diff[0][:], neg_z0[:], neg_y[0][:], ALU.subtract)
            else:
                nc.vector.tensor_reduce(neg_max_z[1][:], z[1][:], mybir.AxisListType.X, ALU.max, negate=True)
            nc.scalar.activation(summed[i][:], y[i][:], ACT.Exp, bias=neg_max_y[i][:], accum_out=sum_y[i][:])
            nc.scalar.activation(summed[i][:], z[i][:], ACT.Exp, bias=neg_max_z[i][:], accum_out=sum_z[i][:])
            nc.scalar.activation(guess_y[i][:], sum_y[i][:].bitcast(U32), ACT.Copy, scale=LOG_PER_BIT)
            nc.scalar.activation(inv_guess[i][:], sum_z[i][:].bitcast(U32), ACT.Exp, scale=-LOG_PER_BIT, bias=guess_y[i][:])
        for i in range(TILES):
            nc.vector.reciprocal(inv_sum_y[i][:], sum_y[i][:])
            nc.vector.tensor_scalar(known[i][:], neg_max_y[i][:], neg_max_z[i][:], guess_y[i][:], ALU.subtract, ALU.subtract)

        for i in range(TILES):
            added = horner[i][:, DEGREE : DEGREE + 1]
            if i == 0:
                nc.vector.tensor_scalar(ratio[0][:], sum_z[0][:], inv_sum_y[0][:], None, ALU.mult)
                nc.vector.tensor_scalar(added, sum_z[0][:].bitcast(I32), LOG_PER_BIT, known[0][:], ALU.mult, ALU.add)
            else:
                nc.scalar.activation(ratio[1][:], sum_z[1][:], ACT.Copy, scale=inv_sum_y[1][:])
                nc.scalar.activation(added, sum_z[1][:].bitcast(U32), ACT.Identity, scale=LOG_PER_BIT, bias=known[1][:])
            steps = DEGREE + 1 + i
            nc.vector.tensor_scalar(rest[i][:, : DEGREE + 1], inv_guess[i][:].to_broadcast([P, DEGREE + 1]), ratio[i][:], -1.0, ALU.mult, ALU.add)
            nc.vector.tensor_tensor_scan(series[i][:, :steps], rest[i][:, :steps], horner[i][:, :steps], 0.0, ALU.mult, ALU.add)
            if i == 0:
                nc.vector.scalar_tensor_tensor(diff[1][:], z[1][:], -1.0, neg_y[1][:], ALU.mult, ALU.subtract)
        offset = [series[i][:, DEGREE : DEGREE + 1] for i in range(TILES)]

        nc.scalar.activation(summed[0][:], diff[0][:], ACT.Abs, bias=offset[0], accum_out=abs_sum[0][:])
        nc.scalar.activation(summed[1][:], diff[1][:], ACT.Abs, scale=MEAN_SHARE, bias=series[1][:, DEGREE + 1 :], accum_out=abs_sum[1][:])
        nc.vector.tensor_scalar(shift0[:], abs_sum[0][:], -MEAN_SHARE, offset[0], ALU.mult, ALU.add)
        nc.vector.tensor_scalar(reward1[:], diff[1][:], offset[1], None, ALU.add)
        centred = ((diff[0], ALU.add, shift0), (reward1, ALU.subtract, abs_sum[1]))

        width = S // PARTS
        for i in range(TILES):
            values, op, row_term = centred[i]
            for part in range(PARTS):
                cols = slice(part * width, (part + 1) * width)
                nc.vector.scalar_tensor_tensor(arg[i][:, cols], values[:, cols], row_term[:], good_sb[:, cols], op, ALU.mult)
                nc.scalar.activation(tanh[i][:, cols], arg[i][:, cols], ACT.Tanh, scale=-0.75)
        for i in range(TILES):
            for part in range(PARTS):
                cols = slice(part * width, (part + 1) * width)
                nc.vector.scalar_tensor_tensor(res[i][:, cols], tanh[i][:, cols], 1.0, half_lam[:, cols], ALU.add, ALU.mult)
                nc.sync.dma_start(out[i * P : (i + 1) * P, cols], res[i][:, cols])
